import numpy as np
import ml_dtypes


def mxq(x, axis, fmt="e4m3"):
    dtype, down = {"e4m3": (ml_dtypes.float8_e4m3fn, 7), "e5m2": (ml_dtypes.float8_e5m2, 14)}[fmt]
    v = np.moveaxis(np.asarray(x, np.float32).astype(ml_dtypes.bfloat16).astype(np.float64), axis, -1)
    blocks = v.reshape(v.shape[:-1] + (-1, 32))
    amax = np.abs(blocks).max(-1, keepdims=True)
    byte = np.maximum(np.where(amax > 0, np.frexp(amax)[1] - 1 + 127, 0) - down, 1)
    scale = np.exp2(byte - 127.0)
    codes = (blocks / scale).astype(np.float32).astype(dtype).astype(np.float64)
    return np.moveaxis((codes * scale).reshape(v.shape), -1, axis)


WIDE = False


def mx_kscale(k):
    if not WIDE:
        return np.ones(k)
    levels = np.array([10, -10, 5, -5, 0])
    if k % 512:
        return np.exp2(np.random.permutation(np.resize(levels, k // 32))).repeat(32)
    a = np.empty((k // 512, 16))
    for p in range(k // 512):
        a[p, :8] = np.random.permutation(np.resize(levels, 8))
        for g in range(8):
            far = levels[np.abs(levels - a[p, g]) >= 10]
            a[p, g + 8] = far[np.random.randint(len(far))]
    return np.exp2(a.ravel()).repeat(32)


BF16 = ml_dtypes.bfloat16


def bf(x):
    return np.asarray(x, np.float32).astype(BF16)


def f64(x):
    return np.asarray(x).astype(np.float64)


E2M1 = np.array([0.0, 0.5, 1.0, 1.5, 2.0, 3.0, 4.0, 6.0, -0.0, -0.5, -1.0, -1.5, -2.0, -3.0, -4.0, -6.0])


def pack_weight(w, fmt):
    k, n = w.shape
    w = f64(bf(w)).reshape(k // 32, 32, n)
    amax = np.abs(w).max(1)
    if fmt == "e4m3":
        byte = np.frexp(amax)[1] - 1 + 127 - 7
    else:
        mant, ex = np.frexp(amax / 6.0)
        byte = np.where(mant > 0.5, ex, ex - 1) + 127
    byte = np.clip(np.where(amax > 0, byte, 1), 1, 254)
    scaled = (w * np.exp2(127.0 - byte)[:, None, :]).reshape(k, n).astype(np.float32)
    by_word = np.ascontiguousarray(scaled.reshape(k // 512, 128, 4, n).transpose(0, 1, 3, 2))
    if fmt == "e4m3":
        words = by_word.astype(ml_dtypes.float8_e4m3fn).view(np.uint8)
    else:
        c = by_word.astype(ml_dtypes.float4_e2m1fn).view(np.uint8) & 0xF
        words = c[..., 0::2] | (c[..., 1::2] << 4)
    return np.ascontiguousarray(words), np.ascontiguousarray(byte.astype(np.uint8).reshape(k // 512, 16, n))


def unpack_weight(words, scales, fmt):
    g, p, n, _ = words.shape
    if fmt == "e4m3":
        vals = np.ascontiguousarray(words).view(ml_dtypes.float8_e4m3fn).astype(np.float64)
    else:
        nib = np.empty((g, p, n, 4), np.uint8)
        nib[..., 0::2] = words & 0xF
        nib[..., 1::2] = words >> 4
        vals = E2M1[nib]
    vals = vals * np.repeat(np.exp2(scales.astype(np.float64) - 127.0), 8, axis=1)[..., None]
    return vals.transpose(0, 1, 3, 2).reshape(g * 512, n)
def pack4(w):
    words, scales = pack_weight(w, "e2m1")
    return words.reshape(words.shape[0], 128, -1), scales


def unpack4(words, scales):
    return unpack_weight(words.reshape(words.shape[0], 128, -1, 2), scales, "e2m1")


M, N, R = 2048, 3072, 256

NOISE = 0.5


def draw0():
    s, t = mx_kscale(M), mx_kscale(N)
    A = np.random.standard_normal((M, N)) / np.sqrt(M)
    at_words, at_scales = pack4(A.T / t[:, None])
    return {"a": bf(A * s[:, None]),
            "omega": bf(np.random.standard_normal((M, R)) / s[:, None]),
            "sample_w": bf((1 + 0.1 * np.random.standard_normal(N)) * t),
            "noise_var": bf(NOISE * (1 + 0.1 * np.random.standard_normal(M)) * s),
            "at_words": at_words,
            "at_scales": at_scales}


def core(a, omega, sample_w, noise_var, at_words, at_scales):
    om = f64(omega)
    z = mxq(f64(a), 0, "e4m3").T @ mxq(om, 0, "e4m3")
    zw = z * f64(sample_w)[:, None]
    y = unpack4(at_words, at_scales).T @ mxq(zw, 0, "e4m3")
    return y - f64(noise_var)[:, None] * om


def e4m3fn_bytes(y):
    return np.clip(np.asarray(y, np.float64), -448.0, 448.0).astype(np.float32).astype(ml_dtypes.float8_e4m3fn).view(np.uint8)


def e4m3fn_values(b):
    return np.asarray(b, np.uint8).view(ml_dtypes.float8_e4m3fn).astype(np.float64)


def setup_inputs():
    d = draw0()
    x0 = np.asarray(d['a']).astype(np.float64)
    s = (np.max(np.abs(x0), axis=(1,), keepdims=True) / 448.0).astype(np.float32)
    out = {}
    for k, v in d.items():
        if k == 'a':
            out['a_bytes'] = e4m3fn_bytes(x0 / s.astype(np.float64))
            out['a_scale'] = s
        else:
            out[k] = v
    return out


def reference(a_bytes, a_scale, omega, sample_w, noise_var, at_words, at_scales):
    return core(e4m3fn_values(a_bytes) * a_scale.astype(np.float64), omega, sample_w, noise_var, at_words, at_scales)

@@ -1,0 +1,224 @@
+from contextlib import ExitStack
+
+import concourse.mybir as mybir
+from concourse.masks import make_identity
+
+M, N, R = 2048, 3072, 256
+FLOPS = 2 * 2 * M * N * R
+
+F32 = mybir.dt.float32
+BF16 = mybir.dt.bfloat16
+U32 = mybir.dt.uint32
+I32 = mybir.dt.int32
+U8 = mybir.dt.uint8
+FP8 = mybir.dt.float8_e4m3fn
+FP8X4 = mybir.dt.float8_e4m3fn_x4
+FP4X4 = mybir.dt.float4_e2m1fn_x4
+MULT = mybir.AluOpType.mult
+ADD = mybir.AluOpType.add
+
+P = 128
+PACK = 4
+KG = M // 512
+NG = N // 512
+S = 512
+MT = M // P
+NACC = 6
+
+UNITS = NG * KG
+V_BLOCKS = {0: 32, 23: 32}
+
+
+def tile_weighted_range_power_step_s13_kernel(
+    tc, a_bytes, a_scale, omega, sample_w, noise_var, at_words, at_scales, out
+):
+    nc = tc.nc
+    with ExitStack() as ctx:
+        keep = ctx.enter_context(tc.tile_pool(name="keep", bufs=1))
+        work = ctx.enter_context(tc.tile_pool(name="work", bufs=3))
+        psum = ctx.enter_context(tc.psum_pool(name="psum", bufs=1))
+        ctx.enter_context(tc.manual_schedule())
+
+        a_raw = [keep.tile([P, KG, PACK, S], U8, name="a_raw%d" % g, align_bytes=64) for g in range(NG)]
+        om_raw = [keep.tile([P, PACK, R], BF16, name="om_raw%d" % k, align_bytes=64) for k in range(KG)]
+        om_codes = [keep.tile([P, R], U32, name="om_codes%d" % k, align_bytes=64) for k in range(KG)]
+        om_scales = [keep.tile([P, R], U8, name="om_scales%d" % k, align_bytes=64) for k in range(KG)]
+        v_codes = [keep.tile([P, R], U32, name="v_codes%d" % g, align_bytes=64) for g in range(NG)]
+        v_scales = [keep.tile([P, R], U8, name="v_scales%d" % g, align_bytes=64) for g in range(NG)]
+        b_words = [keep.tile([P, 2 * M], U8, name="b_words%d" % g, align_bytes=64) for g in range(NG)]
+        b_scales = keep.tile([P, NG, M], U8, name="b_scales", align_bytes=64)
+        om_rows = keep.tile([P, MT, R], BF16, name="om_rows", align_bytes=64)
+        asc = keep.tile([P, KG, PACK], F32, name="asc")
+        w_sb = keep.tile([P, NG, PACK], BF16, name="w_sb")
+        nz = keep.tile([P, P], BF16, name="nz")
+        ident = keep.tile([P, P], BF16, name="ident")
+        neg_noise = keep.tile([P, MT], F32, name="neg_noise")
+
+        a_view = a_bytes.rearrange("(k p j) (g s) -> g p k j s", p=P, j=PACK, s=S)
+        om_view = omega.rearrange("(k p j) r -> k p j r", p=P, j=PACK)
+
+        def load_a(g):
+            for k in range(KG):
+                nc.sync.dma_start(out=a_raw[g][:, k], in_=a_view[g][:, k])
+
+        nc.vector.memset(b_scales[:].rearrange("p g n -> p (g n)").bitcast(I32), 0)
+        nc.gpsimd.memset(nz[:], 0.0)
+        make_identity(nc, ident[:])
+
+        nc.sync.dma_start(out=asc[:], in_=a_scale.rearrange("(k p j) o -> p k (j o)", p=P, j=PACK))
+        for k in range(KG):
+            nc.sync.dma_start(out=a_raw[0][:, k], in_=a_view[0][:, k])
+            nc.sync.dma_start(out=om_raw[k][:], in_=om_view[k])
+        nc.sync.dma_start(out=nz[0:MT, :], in_=noise_var.rearrange("(m p) -> m p", p=P))
+        nc.sync.dma_start(out=w_sb[:], in_=sample_w.rearrange("(g p j) -> p g j", p=P, j=PACK))
+        load_a(1)
+        s_view = at_scales.bitcast(I32).rearrange("g q n -> q g n")
+        for q in range(4):
+            nc.sync.dma_start(out=b_scales[32 * q : 32 * q + 4].bitcast(I32), in_=s_view[4 * q : 4 * q + 4])
+        for g in range(NG):
+            nc.sync.dma_start(out=b_words[g][:], in_=at_words[g])
+            if g + 2 < NG:
+                load_a(g + 2)
+            if g == 3:
+                nc.sync.dma_start(out=om_rows[:], in_=omega.rearrange("(m p) r -> p m r", p=P))
+
+        planes, grouped, a_codes, a_scales = {}, {}, {}, {}
+        z, acc, v_grouped = {}, {}, {}
+
+        def widen(u):
+            g, k = divmod(u, KG)
+            wide = work.tile([P, PACK, S], BF16, name="wide", bufs=4, align_bytes=64)
+            planes[u] = wide
+            for j in range(PACK):
+                nc.vector.tensor_scalar(
+                    wide[:, j, :], a_raw[g][:, k, j, :].bitcast(FP8), asc[:, k, j : j + 1], None, MULT
+                )
+
+        def interleave(u):
+            wide = planes.pop(u)
+            dst_tile = work.tile([P, S * PACK], BF16, name="dst_tile", bufs=4, align_bytes=64)
+            grouped[u] = dst_tile
+            src = wide[:].rearrange("p j (m i t) -> p m j i t", i=2, t=PACK)
+            dst = dst_tile[:].rearrange("p (t m i j) -> p m j i t", t=PACK, i=2, j=PACK)
+            cut = S // 8 - V_BLOCKS.get(u, 0)
+            if cut > 0:
+                nc.scalar.copy(dst[:, :cut], src[:, :cut])
+            if cut < S // 8:
+                nc.vector.tensor_copy(dst[:, cut:], src[:, cut:])
+
+        def quantize_a(u):
+            codes = work.tile([P, S], U32, name="codes", bufs=6, align_bytes=64)
+            scales = work.tile([P, S], U8, name="scales", bufs=6, align_bytes=64)
+            a_codes[u], a_scales[u] = codes, scales
+            nc.vector.quantize_mx(codes[:].bitcast(FP8X4), scales[:], grouped.pop(u)[:])
+
+        def omega_group(k):
+            om_grouped = work.tile([P, R * PACK], BF16, name="om_grouped", bufs=2, align_bytes=64)
+            nc.vector.tensor_copy(
+                om_grouped[:].rearrange("p (c i j) -> p c j i", i=8, j=PACK),
+                om_raw[k][:].rearrange("p j (c i) -> p c j i", i=8),
+            )
+            return om_grouped
+
+        def omega_quantize(k, om_grouped):
+            nc.vector.quantize_mx(om_codes[k][:].bitcast(FP8X4), om_scales[k][:], om_grouped[:])
+
+        def project(u):
+            g, k = divmod(u, KG)
+            codes, scales = a_codes.pop(u), a_scales.pop(u)
+            for h in range(2):
+                if k == 0:
+                    z[g, h] = psum.tile([P, PACK, P], F32, name="z%d_%d" % (g, h), tag="z%d" % h)
+                for t in range(PACK):
+                    nc.tensor.matmul_mx(
+                        out=z[g, h][:, t, :],
+                        lhsT=codes[:, P * t : P * (t + 1)].bitcast(FP8X4),
+                        lhsT_scale=scales[:, P * t : P * (t + 1)],
+                        rhs=om_codes[k][:, P * h : P * (h + 1)].bitcast(FP8X4),
+                        rhs_scale=om_scales[k][:, P * h : P * (h + 1)],
+                        start=(k == 0 and t == 0),
+                        stop=(k == KG - 1 and t == PACK - 1),
+                    )
+
+        def weigh(g):
+            v_grouped[g] = work.tile([P, R * PACK], BF16, name="v_grouped", bufs=2, align_bytes=64)
+            for h in range(2):
+                nc.vector.tensor_tensor(
+                    v_grouped[g][:, P * PACK * h : P * PACK * (h + 1)].rearrange("p (n j) -> p n j", j=PACK),
+                    z[g, h][:].rearrange("p j n -> p n j"),
+                    w_sb[:, g : g + 1, :].to_broadcast([P, P, PACK]),
+                    MULT,
+                )
+
+        def quantize_v(g):
+            nc.vector.quantize_mx(v_codes[g][:].bitcast(FP8X4), v_scales[g][:], v_grouped[g][:])
+
+        def back(bank, g, m, h, first, last):
+            nc.tensor.matmul_mx(
+                out=acc[bank][:, m % 2, P * h : P * (h + 1)],
+                lhsT=b_words[g][:, 2 * P * m : 2 * P * (m + 1)].bitcast(FP4X4),
+                lhsT_scale=b_scales[:, g, P * m : P * (m + 1)],
+                rhs=v_codes[g][:, P * h : P * (h + 1)].bitcast(FP8X4),
+                rhs_scale=v_scales[g][:, P * h : P * (h + 1)],
+                start=first,
+                stop=last,
+            )
+
+        def back_bank(bank, g):
+            if g == 0:
+                tag = "acc%d" % bank if bank < NACC else "z%d" % (bank - NACC)
+                acc[bank] = psum.tile([P, 2, R], F32, name="acc_%d" % bank, tag=tag)
+            for i in range(2):
+                for h in range(2):
+                    back(bank, g, 2 * bank + i, h, g == 0 and i == 0 and h == 0, g == NG - 1 and i == 1 and h == 1)
+
+        out_view = out.rearrange("(b i p) r -> b p i r", i=2, p=P)
+
+        def finish(bank):
+            y = work.tile([P, 2, R], F32, name="y", bufs=4)
+            for i in range(2):
+                m = 2 * bank + i
+                nc.vector.scalar_tensor_tensor(
+                    y[:, i, :], om_rows[:, m, :], neg_noise[:, m : m + 1], acc[bank][:, i, :], MULT, ADD
+                )
+            nc.sync.dma_start(out=out_view[bank], in_=y[:])
+
+        for s in range(UNITS + 2):
+            if s < UNITS:
+                widen(s)
+                interleave(s)
+            if s < KG:
+                om_grouped = omega_group(s)
+            g_done, phase = divmod(s - 2, KG)
+            if phase == 0 and g_done > 0:
+                weigh(g_done - 1)
+            if s >= 2:
+                quantize_a(s - 2)
+            if s < KG:
+                omega_quantize(s, om_grouped)
+            if phase == 0 and g_done > 0:
+                quantize_v(g_done - 1)
+            if s == 4:
+                noise_t = psum.tile([P, P], BF16, name="noise_t", tag="acc5")
+                nc.tensor.transpose(noise_t[:], nz[:], ident[:])
+                nc.vector.tensor_scalar(neg_noise[:], noise_t[:, 0:MT], -1.0, None, MULT)
+            if s >= 2:
+                project(s - 2)
+                if g_done > 0:
+                    banks = ((0, 1), (2, 3), (4,), (5,))[phase]
+                    for bank in banks:
+                        back_bank(bank, g_done - 1)
+
+        last = NG - 1
+        weigh(last)
+        quantize_v(last)
+        for g in range(last):
+            back_bank(NACC, g)
+        for bank in range(NACC):
+            back_bank(bank, last)
+            finish(bank)
+        back_bank(NACC, last)
+        finish(NACC)
+        for g in range(NG):
+            back_bank(NACC + 1, g)
+        finish(NACC + 1)

@@ -16,6 +16,7 @@ FP8X4 = mybir.dt.float8_e4m3fn_x4
 FP4X4 = mybir.dt.float4_e2m1fn_x4
 MULT = mybir.AluOpType.mult
 ADD = mybir.AluOpType.add
+COPY = mybir.ActivationFunctionType.Copy
 
 P = 128
 PACK = 4
@@ -23,10 +24,15 @@ KG = M // 512
 NG = N // 512
 S = 512
 MT = M // P
+PAIRS = MT // 2
 NACC = 6
+LATE = (6, 7)
+LAST = NG - 1
 
 UNITS = NG * KG
-V_BLOCKS = {0: 32, 23: 32}
+BLOCKS = S // 8
+V_BLOCKS = {0: 32, 8: 32, 16: 32, 22: 16, 23: 40}
+S_PLANES = {0: (3,)}
 
 
 def tile_weighted_range_power_step_s13_kernel(
@@ -39,7 +45,11 @@ def tile_weighted_range_power_step_s13_kernel(
         psum = ctx.enter_context(tc.psum_pool(name="psum", bufs=1))
         ctx.enter_context(tc.manual_schedule())
 
-        a_raw = [keep.tile([P, KG, PACK, S], U8, name="a_raw%d" % g, align_bytes=64) for g in range(NG)]
+        a_raw = {
+            (g, k): keep.tile([P, PACK, S], U8, name="a_raw%d_%d" % (g, k), align_bytes=64)
+            for g in range(NG)
+            for k in range(KG)
+        }
         om_raw = [keep.tile([P, PACK, R], BF16, name="om_raw%d" % k, align_bytes=64) for k in range(KG)]
         om_codes = [keep.tile([P, R], U32, name="om_codes%d" % k, align_bytes=64) for k in range(KG)]
         om_scales = [keep.tile([P, R], U8, name="om_scales%d" % k, align_bytes=64) for k in range(KG)]
@@ -54,63 +64,97 @@ def tile_weighted_range_power_step_s13_kernel(
         ident = keep.tile([P, P], BF16, name="ident")
         neg_noise = keep.tile([P, MT], F32, name="neg_noise")
 
-        a_view = a_bytes.rearrange("(k p j) (g s) -> g p k j s", p=P, j=PACK, s=S)
+        a_view = a_bytes.rearrange("(k p j) n -> k p j n", p=P, j=PACK)
         om_view = omega.rearrange("(k p j) r -> k p j r", p=P, j=PACK)
+        scale_view = at_scales.bitcast(I32).rearrange("g q n -> q g n")
 
-        def load_a(g):
-            for k in range(KG):
-                nc.sync.dma_start(out=a_raw[g][:, k], in_=a_view[g][:, k])
+        def load_a(g, k):
+            nc.sync.dma_start(out=a_raw[g, k][:], in_=a_view[k][:, :, S * g : S * (g + 1)])
 
+        def load_om(k):
+            nc.sync.dma_start(out=om_raw[k][:], in_=om_view[k])
+
+        def load_bs(q):
+            nc.sync.dma_start(out=b_scales[32 * q : 32 * q + 4].bitcast(I32), in_=scale_view[4 * q : 4 * q + 4])
+
+        def load_b(g):
+            nc.sync.dma_start(out=b_words[g][:], in_=at_words[g])
+
+        nc.scalar.dma_start(out=asc[:], in_=a_scale.rearrange("(k p j) o -> p k (j o)", p=P, j=PACK))
         nc.vector.memset(b_scales[:].rearrange("p g n -> p (g n)").bitcast(I32), 0)
         nc.gpsimd.memset(nz[:], 0.0)
         make_identity(nc, ident[:])
 
-        nc.sync.dma_start(out=asc[:], in_=a_scale.rearrange("(k p j) o -> p k (j o)", p=P, j=PACK))
-        for k in range(KG):
-            nc.sync.dma_start(out=a_raw[0][:, k], in_=a_view[0][:, k])
-            nc.sync.dma_start(out=om_raw[k][:], in_=om_view[k])
+        load_a(0, 0)
+        load_om(0)
+        load_a(0, 1)
+        load_om(1)
+        load_a(0, 2)
+        load_a(0, 3)
+        load_om(2)
+        load_om(3)
+        load_a(1, 0)
+        load_a(1, 1)
         nc.sync.dma_start(out=nz[0:MT, :], in_=noise_var.rearrange("(m p) -> m p", p=P))
         nc.sync.dma_start(out=w_sb[:], in_=sample_w.rearrange("(g p j) -> p g j", p=P, j=PACK))
-        load_a(1)
-        s_view = at_scales.bitcast(I32).rearrange("g q n -> q g n")
-        for q in range(4):
-            nc.sync.dma_start(out=b_scales[32 * q : 32 * q + 4].bitcast(I32), in_=s_view[4 * q : 4 * q + 4])
-        for g in range(NG):
-            nc.sync.dma_start(out=b_words[g][:], in_=at_words[g])
-            if g + 2 < NG:
-                load_a(g + 2)
-            if g == 3:
-                nc.sync.dma_start(out=om_rows[:], in_=omega.rearrange("(m p) r -> p m r", p=P))
+        load_a(1, 2)
+        load_a(1, 3)
+        load_bs(0)
+        load_a(2, 0)
+        load_bs(1)
+        load_a(2, 1)
+        load_bs(2)
+        load_a(2, 2)
+        load_bs(3)
+        load_a(2, 3)
+        load_b(0)
+        load_a(3, 0)
+        load_a(3, 1)
+        load_b(1)
+        load_a(3, 2)
+        load_a(3, 3)
+        load_b(2)
+        load_a(4, 0)
+        load_a(4, 1)
+        load_a(4, 2)
+        load_a(4, 3)
+        load_b(3)
+        load_b(4)
+        nc.sync.dma_start(out=om_rows[:], in_=omega.rearrange("(m p) r -> p m r", p=P))
+        load_a(5, 0)
+        load_a(5, 1)
+        load_a(5, 2)
+        load_a(5, 3)
+        load_b(5)
 
         planes, grouped, a_codes, a_scales = {}, {}, {}, {}
         z, acc, v_grouped = {}, {}, {}
 
         def widen(u):
             g, k = divmod(u, KG)
-            wide = work.tile([P, PACK, S], BF16, name="wide", bufs=4, align_bytes=64)
-            planes[u] = wide
+            planes[u] = work.tile([P, PACK, S], BF16, name="wide", bufs=4, align_bytes=64)
             for j in range(PACK):
-                nc.vector.tensor_scalar(
-                    wide[:, j, :], a_raw[g][:, k, j, :].bitcast(FP8), asc[:, k, j : j + 1], None, MULT
-                )
+                in_ = a_raw[g, k][:, j, :].bitcast(FP8)
+                if j in S_PLANES.get(u, ()):
+                    nc.scalar.activation(planes[u][:, j, :], in_, COPY, scale=asc[:, k, j : j + 1])
+                else:
+                    nc.vector.tensor_scalar(planes[u][:, j, :], in_, asc[:, k, j : j + 1], None, MULT)
 
         def interleave(u):
             wide = planes.pop(u)
-            dst_tile = work.tile([P, S * PACK], BF16, name="dst_tile", bufs=4, align_bytes=64)
-            grouped[u] = dst_tile
+            grouped[u] = work.tile([P, S * PACK], BF16, name="dst_tile", bufs=4, align_bytes=64)
             src = wide[:].rearrange("p j (m i t) -> p m j i t", i=2, t=PACK)
-            dst = dst_tile[:].rearrange("p (t m i j) -> p m j i t", t=PACK, i=2, j=PACK)
-            cut = S // 8 - V_BLOCKS.get(u, 0)
+            dst = grouped[u][:].rearrange("p (t m i j) -> p m j i t", t=PACK, i=2, j=PACK)
+            cut = BLOCKS - V_BLOCKS.get(u, 0)
             if cut > 0:
                 nc.scalar.copy(dst[:, :cut], src[:, :cut])
-            if cut < S // 8:
+            if cut < BLOCKS:
                 nc.vector.tensor_copy(dst[:, cut:], src[:, cut:])
 
         def quantize_a(u):
-            codes = work.tile([P, S], U32, name="codes", bufs=6, align_bytes=64)
-            scales = work.tile([P, S], U8, name="scales", bufs=6, align_bytes=64)
-            a_codes[u], a_scales[u] = codes, scales
-            nc.vector.quantize_mx(codes[:].bitcast(FP8X4), scales[:], grouped.pop(u)[:])
+            a_codes[u] = work.tile([P, S], U32, name="codes", bufs=6, align_bytes=64)
+            a_scales[u] = work.tile([P, S], U8, name="scales", bufs=6, align_bytes=64)
+            nc.vector.quantize_mx(a_codes[u][:].bitcast(FP8X4), a_scales[u][:], grouped.pop(u)[:])
 
         def omega_group(k):
             om_grouped = work.tile([P, R * PACK], BF16, name="om_grouped", bufs=2, align_bytes=64)
@@ -140,22 +184,32 @@ def tile_weighted_range_power_step_s13_kernel(
                         stop=(k == KG - 1 and t == PACK - 1),
                     )
 
+        HALF = P * PACK
+
         def weigh(g):
             v_grouped[g] = work.tile([P, R * PACK], BF16, name="v_grouped", bufs=2, align_bytes=64)
             for h in range(2):
                 nc.vector.tensor_tensor(
-                    v_grouped[g][:, P * PACK * h : P * PACK * (h + 1)].rearrange("p (n j) -> p n j", j=PACK),
+                    v_grouped[g][:, HALF * h : HALF * (h + 1)].rearrange("p (n j) -> p n j", j=PACK),
                     z[g, h][:].rearrange("p j n -> p n j"),
                     w_sb[:, g : g + 1, :].to_broadcast([P, P, PACK]),
                     MULT,
                 )
 
-        def quantize_v(g):
-            nc.vector.quantize_mx(v_codes[g][:].bitcast(FP8X4), v_scales[g][:], v_grouped[g][:])
+        def quantize_v(g, pieces):
+            width = R // pieces
+            for i in range(pieces):
+                cols = slice(width * i, width * (i + 1))
+                nc.vector.quantize_mx(
+                    v_codes[g][:, cols].bitcast(FP8X4),
+                    v_scales[g][:, cols],
+                    v_grouped[g][:, PACK * width * i : PACK * width * (i + 1)],
+                )
 
-        def back(bank, g, m, h, first, last):
+        def back(pair, g, i, h, first, last):
+            m = 2 * pair + i
             nc.tensor.matmul_mx(
-                out=acc[bank][:, m % 2, P * h : P * (h + 1)],
+                out=acc[pair][:, i, P * h : P * (h + 1)],
                 lhsT=b_words[g][:, 2 * P * m : 2 * P * (m + 1)].bitcast(FP4X4),
                 lhsT_scale=b_scales[:, g, P * m : P * (m + 1)],
                 rhs=v_codes[g][:, P * h : P * (h + 1)].bitcast(FP8X4),
@@ -164,61 +218,71 @@ def tile_weighted_range_power_step_s13_kernel(
                 stop=last,
             )
 
-        def back_bank(bank, g):
-            if g == 0:
-                tag = "acc%d" % bank if bank < NACC else "z%d" % (bank - NACC)
-                acc[bank] = psum.tile([P, 2, R], F32, name="acc_%d" % bank, tag=tag)
-            for i in range(2):
-                for h in range(2):
-                    back(bank, g, 2 * bank + i, h, g == 0 and i == 0 and h == 0, g == NG - 1 and i == 1 and h == 1)
+        def back_pair(pair, g, tag=None):
+            if tag is not None:
+                acc[pair] = psum.tile([P, 2, R], F32, name="acc%d_%d" % (pair, g), tag=tag)
+            closes = g == LAST
+            for h in range(2):
+                for i in range(2):
+                    back(pair, g, i, h, tag is not None and h == 0 and i == 0, closes and h == 1 and i == 1)
 
         out_view = out.rearrange("(b i p) r -> b p i r", i=2, p=P)
+        y = {}
 
-        def finish(bank):
-            y = work.tile([P, 2, R], F32, name="y", bufs=4)
+        def subtract(m, result):
+            nc.vector.scalar_tensor_tensor(
+                result, om_rows[:, m, :], neg_noise[:, m : m + 1], acc[m // 2][:, m % 2, :], MULT, ADD
+            )
+
+        def finish(pair):
+            y[pair] = work.tile([P, 2, R], F32, name="y", bufs=8)
             for i in range(2):
-                m = 2 * bank + i
-                nc.vector.scalar_tensor_tensor(
-                    y[:, i, :], om_rows[:, m, :], neg_noise[:, m : m + 1], acc[bank][:, i, :], MULT, ADD
-                )
-            nc.sync.dma_start(out=out_view[bank], in_=y[:])
+                m = 2 * pair + i
+                subtract(m, y[pair][:, i, :])
+            nc.sync.dma_start(out=out_view[pair], in_=y[pair][:])
 
+        to_back = []
+        widen(0)
         for s in range(UNITS + 2):
-            if s < UNITS:
-                widen(s)
-                interleave(s)
-            if s < KG:
-                om_grouped = omega_group(s)
             g_done, phase = divmod(s - 2, KG)
-            if phase == 0 and g_done > 0:
-                weigh(g_done - 1)
+            if s < UNITS:
+                interleave(s)
+            if s + 1 < UNITS:
+                widen(s + 1)
+            om_grouped = omega_group(s - 1) if 1 <= s <= KG else None
+            ready = [g_done - 1] if phase == 0 and g_done > 0 else []
+            for g in ready:
+                weigh(g)
             if s >= 2:
                 quantize_a(s - 2)
-            if s < KG:
-                omega_quantize(s, om_grouped)
-            if phase == 0 and g_done > 0:
-                quantize_v(g_done - 1)
-            if s == 4:
+            if om_grouped is not None:
+                omega_quantize(s - 1, om_grouped)
+            for g in ready:
+                quantize_v(g, 1)
+            if s == 3:
                 noise_t = psum.tile([P, P], BF16, name="noise_t", tag="acc5")
                 nc.tensor.transpose(noise_t[:], nz[:], ident[:])
                 nc.vector.tensor_scalar(neg_noise[:], noise_t[:, 0:MT], -1.0, None, MULT)
             if s >= 2:
                 project(s - 2)
-                if g_done > 0:
-                    banks = ((0, 1), (2, 3), (4,), (5,))[phase]
-                    for bank in banks:
-                        back_bank(bank, g_done - 1)
+            for g in ready:
+                to_back += [(pair, g) for pair in range(NACC)]
+            n_back = 3 if 10 <= s < 25 else 0
+            for pair, g in to_back[:n_back]:
+                back_pair(pair, g, "acc%d" % pair if g == 0 else None)
+            to_back = to_back[n_back:]
 
-        last = NG - 1
-        weigh(last)
-        quantize_v(last)
-        for g in range(last):
-            back_bank(NACC, g)
-        for bank in range(NACC):
-            back_bank(bank, last)
-            finish(bank)
-        back_bank(NACC, last)
-        finish(NACC)
-        for g in range(NG):
-            back_bank(NACC + 1, g)
-        finish(NACC + 1)
+        weigh(LAST)
+        quantize_v(LAST, 2)
+        for pair, g in to_back:
+            back_pair(pair, g)
+        late = [(pair, g) for pair in LATE for g in range(NG)]
+        for pair, g in late[:2]:
+            back_pair(pair, g, "z%d" % (pair - NACC) if g == 0 else None)
+        for pair in range(NACC):
+            back_pair(pair, LAST)
+            finish(pair)
+        for pair, g in late[2:]:
+            back_pair(pair, g, "z%d" % (pair - NACC) if g == 0 else None)
+            if g == LAST:
+                finish(pair)

@@ -31,7 +31,7 @@ LAST = NG - 1
 
 UNITS = NG * KG
 BLOCKS = S // 8
-V_BLOCKS = {0: 32, 8: 32, 16: 32, 22: 16, 23: 40}
+V_BLOCKS = {0: 32, 23: 32}
 S_PLANES = {0: (3,)}
 
 

@@ -31,8 +31,8 @@ LAST = NG - 1
 
 UNITS = NG * KG
 BLOCKS = S // 8
-V_BLOCKS = {0: 32, 23: 32}
-S_PLANES = {0: (3,)}
+V_BLOCKS = {0: 24, 23: 32, 16: 48, 21: 16, 11: 24, 5: 32, 17: 32, 19: 8, 20: 48, 7: 48}
+S_PLANES = {0: (3,), 20: (3,), 2: (2, 3), 12: (3,), 18: (2, 3), 22: (1, 2, 3), 9: (1, 2, 3), 23: (3,), 13: (3,), 21: (3,), 7: (3,)}
 
 
 def tile_weighted_range_power_step_s13_kernel(
@@ -132,7 +132,7 @@ def tile_weighted_range_power_step_s13_kernel(
 
         def widen(u):
             g, k = divmod(u, KG)
-            planes[u] = work.tile([P, PACK, S], BF16, name="wide", bufs=4, align_bytes=64)
+            planes[u] = work.tile([P, PACK, S], BF16, name="wide", bufs=5, align_bytes=64)
             for j in range(PACK):
                 in_ = a_raw[g, k][:, j, :].bitcast(FP8)
                 if j in S_PLANES.get(u, ()):
@@ -143,12 +143,14 @@ def tile_weighted_range_power_step_s13_kernel(
         def interleave(u):
             wide = planes.pop(u)
             grouped[u] = work.tile([P, S * PACK], BF16, name="dst_tile", bufs=4, align_bytes=64)
-            src = wide[:].rearrange("p j (m i t) -> p m j i t", i=2, t=PACK)
-            dst = grouped[u][:].rearrange("p (t m i j) -> p m j i t", t=PACK, i=2, j=PACK)
             cut = BLOCKS - V_BLOCKS.get(u, 0)
             if cut > 0:
+                src = wide[:].rearrange("p j (m i t) -> p m j i t", i=2, t=PACK)
+                dst = grouped[u][:].rearrange("p (t m i j) -> p m j i t", t=PACK, i=2, j=PACK)
                 nc.scalar.copy(dst[:, :cut], src[:, :cut])
             if cut < BLOCKS:
+                src = wide[:].rearrange("p j (m i t) -> p m t i j", i=2, t=PACK)
+                dst = grouped[u][:].rearrange("p (t m i j) -> p m t i j", t=PACK, i=2, j=PACK)
                 nc.vector.tensor_copy(dst[:, cut:], src[:, cut:])
 
         def quantize_a(u):
@@ -159,8 +161,7 @@ def tile_weighted_range_power_step_s13_kernel(
         def omega_group(k):
             om_grouped = work.tile([P, R * PACK], BF16, name="om_grouped", bufs=2, align_bytes=64)
             nc.vector.tensor_copy(
-                om_grouped[:].rearrange("p (c i j) -> p c j i", i=8, j=PACK),
-                om_raw[k][:].rearrange("p j (c i) -> p c j i", i=8),
+                om_grouped[:].rearrange("p (c j) -> p c j", j=PACK), om_raw[k][:].rearrange("p j c -> p c j")
             )
             return om_grouped
 
@@ -241,20 +242,25 @@ def tile_weighted_range_power_step_s13_kernel(
                 subtract(m, y[pair][:, i, :])
             nc.sync.dma_start(out=out_view[pair], in_=y[pair][:])
 
+        AHEAD = 2
+        Q_FIRST = True
         to_back = []
-        widen(0)
+        for u in range(AHEAD):
+            widen(u)
         for s in range(UNITS + 2):
             g_done, phase = divmod(s - 2, KG)
             if s < UNITS:
                 interleave(s)
-            if s + 1 < UNITS:
-                widen(s + 1)
+            if s + AHEAD < UNITS and not Q_FIRST:
+                widen(s + AHEAD)
             om_grouped = omega_group(s - 1) if 1 <= s <= KG else None
             ready = [g_done - 1] if phase == 0 and g_done > 0 else []
             for g in ready:
                 weigh(g)
             if s >= 2:
                 quantize_a(s - 2)
+            if s + AHEAD < UNITS and Q_FIRST:
+                widen(s + AHEAD)
             if om_grouped is not None:
                 omega_quantize(s - 1, om_grouped)
             for g in ready:
@@ -277,12 +283,12 @@ def tile_weighted_range_power_step_s13_kernel(
         for pair, g in to_back:
             back_pair(pair, g)
         late = [(pair, g) for pair in LATE for g in range(NG)]
-        for pair, g in late[:2]:
+        for pair, g in late[:3]:
             back_pair(pair, g, "z%d" % (pair - NACC) if g == 0 else None)
         for pair in range(NACC):
             back_pair(pair, LAST)
             finish(pair)
-        for pair, g in late[2:]:
+        for pair, g in late[3:]:
             back_pair(pair, g, "z%d" % (pair - NACC) if g == 0 else None)
             if g == LAST:
                 finish(pair)

from contextlib import ExitStack

import concourse.mybir as mybir
from concourse.masks import make_identity

M, N, R = 2048, 3072, 256
FLOPS = 2 * 2 * M * N * R

F32 = mybir.dt.float32
BF16 = mybir.dt.bfloat16
U32 = mybir.dt.uint32
I32 = mybir.dt.int32
U8 = mybir.dt.uint8
FP8 = mybir.dt.float8_e4m3fn
FP8X4 = mybir.dt.float8_e4m3fn_x4
FP4X4 = mybir.dt.float4_e2m1fn_x4
MULT = mybir.AluOpType.mult
ADD = mybir.AluOpType.add
COPY = mybir.ActivationFunctionType.Copy

P = 128
PACK = 4
KG = M // 512
NG = N // 512
S = 512
MT = M // P
PAIRS = MT // 2
NACC = 6
LATE = (6, 7)
LAST = NG - 1

UNITS = NG * KG
BLOCKS = S // 8
V_BLOCKS = {0: 24, 23: 32, 16: 48, 21: 16, 11: 24, 5: 32, 17: 32, 19: 8, 20: 48, 7: 48}
S_PLANES = {0: (3,), 20: (3,), 2: (2, 3), 12: (3,), 18: (2, 3), 22: (1, 2, 3), 9: (1, 2, 3), 23: (3,), 13: (3,), 21: (3,), 7: (3,)}


def tile_weighted_range_power_step_s13_kernel(
    tc, a_bytes, a_scale, omega, sample_w, noise_var, at_words, at_scales, out
):
    nc = tc.nc
    with ExitStack() as ctx:
        keep = ctx.enter_context(tc.tile_pool(name="keep", bufs=1))
        work = ctx.enter_context(tc.tile_pool(name="work", bufs=3))
        psum = ctx.enter_context(tc.psum_pool(name="psum", bufs=1))
        ctx.enter_context(tc.manual_schedule())

        a_raw = {
            (g, k): keep.tile([P, PACK, S], U8, name="a_raw%d_%d" % (g, k), align_bytes=64)
            for g in range(NG)
            for k in range(KG)
        }
        om_raw = [keep.tile([P, PACK, R], BF16, name="om_raw%d" % k, align_bytes=64) for k in range(KG)]
        om_codes = [keep.tile([P, R], U32, name="om_codes%d" % k, align_bytes=64) for k in range(KG)]
        om_scales = [keep.tile([P, R], U8, name="om_scales%d" % k, align_bytes=64) for k in range(KG)]
        v_codes = [keep.tile([P, R], U32, name="v_codes%d" % g, align_bytes=64) for g in range(NG)]
        v_scales = [keep.tile([P, R], U8, name="v_scales%d" % g, align_bytes=64) for g in range(NG)]
        b_words = [keep.tile([P, 2 * M], U8, name="b_words%d" % g, align_bytes=64) for g in range(NG)]
        b_scales = keep.tile([P, NG, M], U8, name="b_scales", align_bytes=64)
        om_rows = keep.tile([P, MT, R], BF16, name="om_rows", align_bytes=64)
        asc = keep.tile([P, KG, PACK], F32, name="asc")
        w_sb = keep.tile([P, NG, PACK], BF16, name="w_sb")
        nz = keep.tile([P, P], BF16, name="nz")
        ident = keep.tile([P, P], BF16, name="ident")
        neg_noise = keep.tile([P, MT], F32, name="neg_noise")

        a_view = a_bytes.rearrange("(k p j) n -> k p j n", p=P, j=PACK)
        om_view = omega.rearrange("(k p j) r -> k p j r", p=P, j=PACK)
        scale_view = at_scales.bitcast(I32).rearrange("g q n -> q g n")

        def load_a(g, k):
            nc.sync.dma_start(out=a_raw[g, k][:], in_=a_view[k][:, :, S * g : S * (g + 1)])

        def load_om(k):
            nc.sync.dma_start(out=om_raw[k][:], in_=om_view[k])

        def load_bs(q):
            nc.sync.dma_start(out=b_scales[32 * q : 32 * q + 4].bitcast(I32), in_=scale_view[4 * q : 4 * q + 4])

        def load_b(g):
            nc.sync.dma_start(out=b_words[g][:], in_=at_words[g])

        nc.scalar.dma_start(out=asc[:], in_=a_scale.rearrange("(k p j) o -> p k (j o)", p=P, j=PACK))
        nc.vector.memset(b_scales[:].rearrange("p g n -> p (g n)").bitcast(I32), 0)
        nc.gpsimd.memset(nz[:], 0.0)
        make_identity(nc, ident[:])

        load_a(0, 0)
        load_om(0)
        load_a(0, 1)
        load_om(1)
        load_a(0, 2)
        load_a(0, 3)
        load_om(2)
        load_om(3)
        load_a(1, 0)
        load_a(1, 1)
        nc.sync.dma_start(out=nz[0:MT, :], in_=noise_var.rearrange("(m p) -> m p", p=P))
        nc.sync.dma_start(out=w_sb[:], in_=sample_w.rearrange("(g p j) -> p g j", p=P, j=PACK))
        load_a(1, 2)
        load_a(1, 3)
        load_bs(0)
        load_a(2, 0)
        load_bs(1)
        load_a(2, 1)
        load_bs(2)
        load_a(2, 2)
        load_bs(3)
        load_a(2, 3)
        load_b(0)
        load_a(3, 0)
        load_a(3, 1)
        load_b(1)
        load_a(3, 2)
        load_a(3, 3)
        load_b(2)
        load_a(4, 0)
        load_a(4, 1)
        load_a(4, 2)
        load_a(4, 3)
        load_b(3)
        load_b(4)
        nc.sync.dma_start(out=om_rows[:], in_=omega.rearrange("(m p) r -> p m r", p=P))
        load_a(5, 0)
        load_a(5, 1)
        load_a(5, 2)
        load_a(5, 3)
        load_b(5)

        planes, grouped, a_codes, a_scales = {}, {}, {}, {}
        z, acc, v_grouped = {}, {}, {}

        def widen(u):
            g, k = divmod(u, KG)
            planes[u] = work.tile([P, PACK, S], BF16, name="wide", bufs=5, align_bytes=64)
            for j in range(PACK):
                in_ = a_raw[g, k][:, j, :].bitcast(FP8)
                if j in S_PLANES.get(u, ()):
                    nc.scalar.activation(planes[u][:, j, :], in_, COPY, scale=asc[:, k, j : j + 1])
                else:
                    nc.vector.tensor_scalar(planes[u][:, j, :], in_, asc[:, k, j : j + 1], None, MULT)

        def interleave(u):
            wide = planes.pop(u)
            grouped[u] = work.tile([P, S * PACK], BF16, name="dst_tile", bufs=4, align_bytes=64)
            cut = BLOCKS - V_BLOCKS.get(u, 0)
            if cut > 0:
                src = wide[:].rearrange("p j (m i t) -> p m j i t", i=2, t=PACK)
                dst = grouped[u][:].rearrange("p (t m i j) -> p m j i t", t=PACK, i=2, j=PACK)
                nc.scalar.copy(dst[:, :cut], src[:, :cut])
            if cut < BLOCKS:
                src = wide[:].rearrange("p j (m i t) -> p m t i j", i=2, t=PACK)
                dst = grouped[u][:].rearrange("p (t m i j) -> p m t i j", t=PACK, i=2, j=PACK)
                nc.vector.tensor_copy(dst[:, cut:], src[:, cut:])

        def quantize_a(u):
            a_codes[u] = work.tile([P, S], U32, name="codes", bufs=6, align_bytes=64)
            a_scales[u] = work.tile([P, S], U8, name="scales", bufs=6, align_bytes=64)
            nc.vector.quantize_mx(a_codes[u][:].bitcast(FP8X4), a_scales[u][:], grouped.pop(u)[:])

        def omega_group(k):
            om_grouped = work.tile([P, R * PACK], BF16, name="om_grouped", bufs=2, align_bytes=64)
            nc.vector.tensor_copy(
                om_grouped[:].rearrange("p (c j) -> p c j", j=PACK), om_raw[k][:].rearrange("p j c -> p c j")
            )
            return om_grouped

        def omega_quantize(k, om_grouped):
            nc.vector.quantize_mx(om_codes[k][:].bitcast(FP8X4), om_scales[k][:], om_grouped[:])

        def project(u):
            g, k = divmod(u, KG)
            codes, scales = a_codes.pop(u), a_scales.pop(u)
            for h in range(2):
                if k == 0:
                    z[g, h] = psum.tile([P, PACK, P], F32, name="z%d_%d" % (g, h), tag="z%d" % h)
                for t in range(PACK):
                    nc.tensor.matmul_mx(
                        out=z[g, h][:, t, :],
                        lhsT=codes[:, P * t : P * (t + 1)].bitcast(FP8X4),
                        lhsT_scale=scales[:, P * t : P * (t + 1)],
                        rhs=om_codes[k][:, P * h : P * (h + 1)].bitcast(FP8X4),
                        rhs_scale=om_scales[k][:, P * h : P * (h + 1)],
                        start=(k == 0 and t == 0),
                        stop=(k == KG - 1 and t == PACK - 1),
                    )

        HALF = P * PACK

        def weigh(g):
            v_grouped[g] = work.tile([P, R * PACK], BF16, name="v_grouped", bufs=2, align_bytes=64)
            for h in range(2):
                nc.vector.tensor_tensor(
                    v_grouped[g][:, HALF * h : HALF * (h + 1)].rearrange("p (n j) -> p n j", j=PACK),
                    z[g, h][:].rearrange("p j n -> p n j"),
                    w_sb[:, g : g + 1, :].to_broadcast([P, P, PACK]),
                    MULT,
                )

        def quantize_v(g, pieces):
            width = R // pieces
            for i in range(pieces):
                cols = slice(width * i, width * (i + 1))
                nc.vector.quantize_mx(
                    v_codes[g][:, cols].bitcast(FP8X4),
                    v_scales[g][:, cols],
                    v_grouped[g][:, PACK * width * i : PACK * width * (i + 1)],
                )

        def back(pair, g, i, h, first, last):
            m = 2 * pair + i
            nc.tensor.matmul_mx(
                out=acc[pair][:, i, P * h : P * (h + 1)],
                lhsT=b_words[g][:, 2 * P * m : 2 * P * (m + 1)].bitcast(FP4X4),
                lhsT_scale=b_scales[:, g, P * m : P * (m + 1)],
                rhs=v_codes[g][:, P * h : P * (h + 1)].bitcast(FP8X4),
                rhs_scale=v_scales[g][:, P * h : P * (h + 1)],
                start=first,
                stop=last,
            )

        def back_pair(pair, g, tag=None):
            if tag is not None:
                acc[pair] = psum.tile([P, 2, R], F32, name="acc%d_%d" % (pair, g), tag=tag)
            closes = g == LAST
            for h in range(2):
                for i in range(2):
                    back(pair, g, i, h, tag is not None and h == 0 and i == 0, closes and h == 1 and i == 1)

        out_view = out.rearrange("(b i p) r -> b p i r", i=2, p=P)
        y = {}

        def subtract(m, result):
            nc.vector.scalar_tensor_tensor(
                result, om_rows[:, m, :], neg_noise[:, m : m + 1], acc[m // 2][:, m % 2, :], MULT, ADD
            )

        def finish(pair):
            y[pair] = work.tile([P, 2, R], F32, name="y", bufs=8)
            for i in range(2):
                m = 2 * pair + i
                subtract(m, y[pair][:, i, :])
            nc.sync.dma_start(out=out_view[pair], in_=y[pair][:])

        AHEAD = 2
        Q_FIRST = True
        to_back = []
        for u in range(AHEAD):
            widen(u)
        for s in range(UNITS + 2):
            g_done, phase = divmod(s - 2, KG)
            if s < UNITS:
                interleave(s)
            if s + AHEAD < UNITS and not Q_FIRST:
                widen(s + AHEAD)
            om_grouped = omega_group(s - 1) if 1 <= s <= KG else None
            ready = [g_done - 1] if phase == 0 and g_done > 0 else []
            for g in ready:
                weigh(g)
            if s >= 2:
                quantize_a(s - 2)
            if s + AHEAD < UNITS and Q_FIRST:
                widen(s + AHEAD)
            if om_grouped is not None:
                omega_quantize(s - 1, om_grouped)
            for g in ready:
                quantize_v(g, 1)
            if s == 3:
                noise_t = psum.tile([P, P], BF16, name="noise_t", tag="acc5")
                nc.tensor.transpose(noise_t[:], nz[:], ident[:])
                nc.vector.tensor_scalar(neg_noise[:], noise_t[:, 0:MT], -1.0, None, MULT)
            if s >= 2:
                project(s - 2)
            for g in ready:
                to_back += [(pair, g) for pair in range(NACC)]
            n_back = 3 if 10 <= s < 25 else 0
            for pair, g in to_back[:n_back]:
                back_pair(pair, g, "acc%d" % pair if g == 0 else None)
            to_back = to_back[n_back:]

        weigh(LAST)
        quantize_v(LAST, 2)
        for pair, g in to_back:
            back_pair(pair, g)
        late = [(pair, g) for pair in LATE for g in range(NG)]
        for pair, g in late[:3]:
            back_pair(pair, g, "z%d" % (pair - NACC) if g == 0 else None)
        for pair in range(NACC):
            back_pair(pair, LAST)
            finish(pair)
        for pair, g in late[3:]:
            back_pair(pair, g, "z%d" % (pair - NACC) if g == 0 else None)
            if g == LAST:
                finish(pair)
